import numpy as np, ml_dtypes
CORES = [51,54,179,182]
N = 4
import mx_ref
NC = 128
BF = ml_dtypes.bfloat16
def setup_inputs(rng):
    def f(*shape):
        return mx_ref.flush((rng.standard_normal(shape, dtype=np.float32) * np.exp2(rng.integers(-2, 3, shape[:-1] + (1,)))).astype(BF))
    return {"w": f(N, 128, N * 512), "x": f(N, 128, 4 * NC)}
def setup_inputs_blocks(rng):
    d = setup_inputs(rng)
    for k in ("w", "x"): d[k] = mx_ref.spread(d[k], rng, 1)
    return d
def setup_inputs_wide(rng):
    d = setup_inputs(rng)
    for k in ("w", "x"): d[k] = mx_ref.flush((d[k].astype(np.float32) * np.exp2(rng.integers(-8, 9, (N, 1, 1))).astype(np.float32)).astype(BF))
    return d
def setup_inputs_zeros(rng):
    d = setup_inputs(rng); v = d["x"].reshape(N, 128, -1, 4).copy()
    v[np.broadcast_to((rng.random((N, 1, v.shape[2], 1)) < 0.33), v.shape)] = 0
    d["x"] = v.reshape(d["x"].shape)
    return d
def reference(w, x):
    QX = [mx_ref.quantize(x[j]) for j in range(N)]
    y = np.zeros((N, 128, NC), np.float32)
    for r in range(N):
        for j in range(N):
            p = mx_ref.matmul(mx_ref.quantize(w[r][:, 512 * j:512 * j + 512]), QX[j])
            y[r] = p if j == 0 else y[r] + p
    return {"y": y}

@@ -1,0 +1,101 @@
+from concourse.bass import DstId, RemoteDMATransfer
+from concourse.mybir import dt
+
+N = 4
+NC = 128
+
+SCRATCH = {
+    "xb": ("sbuf", [128, 4 * NC], "bfloat16"),
+    "wb": ("sbuf", [128, 4 * NC * N], "bfloat16"),
+    "xq": ("sbuf", [128, NC * N], "float8_e4m3fn_x4"),
+    "xs": ("sbuf", [128, NC * N], "uint8"),
+    "wq": ("sbuf", [128, NC * N], "float8_e4m3fn_x4"),
+    "ws": ("sbuf", [128, NC * N], "uint8"),
+    "acc": ("psum", [128, 512], "float32"),
+    "yb": ("sbuf", [128, NC], "float32"),
+}
+SEMAPHORES = ["xl", "wl", "qx", "qw", "a0", "a1", "a2", "a3", "sent", "mm", "cp", "st"]
+
+
+def _engines(mask):
+    return [1 << i for i in range(mask.bit_length()) if (mask >> i) & 1]
+
+
+def _join(bits):
+    m = 0
+    for b in bits:
+        m |= b
+    return m
+
+
+def _plan(src, cores, topo):
+    def near(c):
+        return topo.host(c) == topo.host(src) and topo.chip(c) == topo.chip(src)
+    on = [c for c in cores if c != src and near(c)]
+    off = [c for c in cores if c != src and not near(c)]
+    off.sort(key=lambda c: topo.die(c) != topo.die(src))
+    leave = topo.mask(src, off[0])
+    for c in off:
+        leave &= topo.mask(src, c)
+    stay = topo.mask(src, on[0])
+    for c in on:
+        stay &= topo.mask(src, c)
+    stay &= ~leave
+    plan = []
+    for group, bits in ((on, _engines(stay)), (off, _engines(leave))):
+        k = len(bits) // len(group)
+        for i, c in enumerate(group):
+            plan.append((c, _join(bits[i * k:(i + 1) * k]), k))
+    return plan
+
+
+def rank_program(g, core, T, topo):
+    rank = T.rank_of(core)
+    if rank is None:
+        return
+    sem = T.sem
+
+    def tile(j):
+        return slice(NC * j, NC * (j + 1))
+
+    own = tile(rank)
+    plan = _plan(core, T.cores, topo)
+
+    g.sync.dma_start(T.xb[:], T.x[:]).then_inc(sem.xl, 16)
+    g.sync.dma_start(T.wb[:], T.w[:]).then_inc(sem.wl, 16)
+
+    g.vector.wait_ge(sem.xl, 16)
+    g.vector.quantize_mx(T.xq[:, own], T.xs[:, own], T.xb[:]).then_inc(sem.qx, 1)
+    g.vector.wait_ge(sem.wl, 16)
+    g.vector.quantize_mx(T.wq[:], T.ws[:], T.wb[:]).then_inc(sem.qw, 1)
+
+    g.wait_ge(sem.qx, 1)
+    left = 0
+    for view in (T.xq[:, own].bitcast(dt.uint8), T.xs[:, own]):
+        transfers = []
+        for dst, mask, k in plan:
+            rid, pid = topo.addr(dst, core)
+            transfers.append(RemoteDMATransfer(dst_ids=[DstId(rid=rid, pnc=pid)], dma_engine_mask=mask,
+                                               remote_sem=sem["a%d" % rank], src=view, dst=view))
+            left += k
+        g.remote_dma_fused(transfers, local_sem=sem.sent)
+
+    g.tensor.wait_ge(sem.qx, 1)
+    g.tensor.wait_ge(sem.qw, 1)
+    order = [core] + [dst for dst, _, _ in plan]
+    for i, c in enumerate(order):
+        j = T.rank_of(c)
+        if c != core:
+            k = [e for dst, _, e in _plan(c, T.cores, topo) if dst == core][0]
+            g.tensor.wait_ge(sem["a%d" % j], 2 * k)
+        mm = g.tensor.matmul_mx(T.acc[:, 0:NC], T.wq[:, tile(j)], T.ws[:, tile(j)], T.xq[:, tile(j)], T.xs[:, tile(j)],
+                                i == 0, i == N - 1)
+    mm.then_inc(sem.mm, 1)
+
+    g.vector.wait_ge(sem.mm, 1)
+    g.vector.tensor_copy(T.yb[:], T.acc[:, 0:NC]).then_inc(sem.cp, 1)
+    g.sync.wait_ge(sem.cp, 1)
+    g.sync.dma_start(T.y[:], T.yb[:]).then_inc(sem.st, 16)
+    g.sync.wait_ge(sem.st, 16)
+
+    g.wait_ge(sem.sent, left)

@@ -14,39 +14,25 @@ SCRATCH = {
     "acc": ("psum", [128, 512], "float32"),
     "yb": ("sbuf", [128, NC], "float32"),
 }
-SEMAPHORES = ["xl", "wl", "qx", "qw", "a0", "a1", "a2", "a3", "sent", "mm", "cp", "st"]
+SEMAPHORES = (["xl", "wl", "qx", "qw", "sent", "mm", "cp", "st"]
+              + ["c%d" % j for j in range(N)]
+              + ["p%d" % j for j in range(N)])
 
 
-def _engines(mask):
-    return [1 << i for i in range(mask.bit_length()) if (mask >> i) & 1]
+def _count(mask):
+    return bin(mask).count("1")
 
 
-def _join(bits):
-    m = 0
-    for b in bits:
-        m |= b
-    return m
-
-
-def _plan(src, cores, topo):
+def _roles(core, cores, topo):
     def near(c):
-        return topo.host(c) == topo.host(src) and topo.chip(c) == topo.chip(src)
-    on = [c for c in cores if c != src and near(c)]
-    off = [c for c in cores if c != src and not near(c)]
-    off.sort(key=lambda c: topo.die(c) != topo.die(src))
-    leave = topo.mask(src, off[0])
-    for c in off:
-        leave &= topo.mask(src, c)
-    stay = topo.mask(src, on[0])
-    for c in on:
-        stay &= topo.mask(src, c)
-    stay &= ~leave
-    plan = []
-    for group, bits in ((on, _engines(stay)), (off, _engines(leave))):
-        k = len(bits) // len(group)
-        for i, c in enumerate(group):
-            plan.append((c, _join(bits[i * k:(i + 1) * k]), k))
-    return plan
+        return topo.host(c) == topo.host(core) and topo.chip(c) == topo.chip(core)
+    peer = [c for c in cores if c != core and near(c)][0]
+    far = [c for c in cores if not near(c)]
+    twin = [c for c in far if topo.die(c) == topo.die(core)][0]
+    cross = [c for c in far if c != twin][0]
+    leave = topo.mask(core, twin) & topo.mask(core, cross)
+    stay = topo.mask(core, peer) & ~leave
+    return peer, twin, cross, leave, stay
 
 
 def rank_program(g, core, T, topo):
@@ -54,40 +40,59 @@ def rank_program(g, core, T, topo):
     if rank is None:
         return
     sem = T.sem
+    peer, twin, cross, leave, stay = _roles(core, T.cores, topo)
+    left = [0]
 
     def tile(j):
         return slice(NC * j, NC * (j + 1))
 
-    own = tile(rank)
-    plan = _plan(core, T.cores, topo)
+    def codes(j):
+        return T.xq[:, tile(j)].bitcast(dt.uint8), sem["c%d" % j]
+
+    def plane(j):
+        return T.xs[:, tile(j)], sem["p%d" % j]
+
+    def send(piece, where):
+        view, arrived = piece
+        transfers = []
+        for dst, mask in where:
+            rid, pid = topo.addr(dst, core)
+            transfers.append(RemoteDMATransfer(dst_ids=[DstId(rid=rid, pnc=pid)], dma_engine_mask=mask,
+                                               remote_sem=arrived, src=view, dst=view))
+            left[0] += _count(mask)
+        g.remote_dma_fused(transfers, local_sem=sem.sent)
 
     g.sync.dma_start(T.xb[:], T.x[:]).then_inc(sem.xl, 16)
     g.sync.dma_start(T.wb[:], T.w[:]).then_inc(sem.wl, 16)
 
     g.vector.wait_ge(sem.xl, 16)
-    g.vector.quantize_mx(T.xq[:, own], T.xs[:, own], T.xb[:]).then_inc(sem.qx, 1)
+    g.vector.quantize_mx(T.xq[:, tile(rank)], T.xs[:, tile(rank)], T.xb[:]).then_inc(sem.qx, 1)
     g.vector.wait_ge(sem.wl, 16)
     g.vector.quantize_mx(T.wq[:], T.ws[:], T.wb[:]).then_inc(sem.qw, 1)
 
+    jt = T.rank_of(twin)
     g.wait_ge(sem.qx, 1)
-    left = 0
-    for view in (T.xq[:, own].bitcast(dt.uint8), T.xs[:, own]):
-        transfers = []
-        for dst, mask, k in plan:
-            rid, pid = topo.addr(dst, core)
-            transfers.append(RemoteDMATransfer(dst_ids=[DstId(rid=rid, pnc=pid)], dma_engine_mask=mask,
-                                               remote_sem=sem["a%d" % rank], src=view, dst=view))
-            left += k
-        g.remote_dma_fused(transfers, local_sem=sem.sent)
+    send(plane(rank), [(twin, leave)])
+    send(codes(rank), [(twin, leave)])
+    send(codes(rank), [(cross, leave), (peer, stay)])
+    send(plane(rank), [(peer, stay)])
+    g.wait_ge(sem["p%d" % jt], _count(_roles(twin, T.cores, topo)[3]))
+    send(plane(jt), [(peer, stay)])
 
+    _, _, _, p_leave, p_stay = _roles(peer, T.cores, topo)
+    _, _, _, t_leave, _ = _roles(twin, T.cores, topo)
+    _, _, _, c_leave, _ = _roles(cross, T.cores, topo)
+    order = [(core, None),
+             (peer, (_count(p_stay), _count(p_stay))),
+             (twin, (_count(t_leave), _count(t_leave))),
+             (cross, (_count(c_leave), _count(p_stay)))]
     g.tensor.wait_ge(sem.qx, 1)
     g.tensor.wait_ge(sem.qw, 1)
-    order = [core] + [dst for dst, _, _ in plan]
-    for i, c in enumerate(order):
+    for i, (c, need) in enumerate(order):
         j = T.rank_of(c)
-        if c != core:
-            k = [e for dst, _, e in _plan(c, T.cores, topo) if dst == core][0]
-            g.tensor.wait_ge(sem["a%d" % j], 2 * k)
+        if need is not None:
+            g.tensor.wait_ge(sem["c%d" % j], need[0])
+            g.tensor.wait_ge(sem["p%d" % j], need[1])
         mm = g.tensor.matmul_mx(T.acc[:, 0:NC], T.wq[:, tile(j)], T.ws[:, tile(j)], T.xq[:, tile(j)], T.xs[:, tile(j)],
                                 i == 0, i == N - 1)
     mm.then_inc(sem.mm, 1)
@@ -98,4 +103,4 @@ def rank_program(g, core, T, topo):
     g.sync.dma_start(T.y[:], T.yb[:]).then_inc(sem.st, 16)
     g.sync.wait_ge(sem.st, 16)
 
-    g.wait_ge(sem.sent, left)
+    g.wait_ge(sem.sent, left[0])

from concourse.bass import DstId, RemoteDMATransfer
from concourse.mybir import dt

N = 4
NC = 128

SCRATCH = {
    "xb": ("sbuf", [128, 4 * NC], "bfloat16"),
    "wb": ("sbuf", [128, 4 * NC * N], "bfloat16"),
    "xq": ("sbuf", [128, NC * N], "float8_e4m3fn_x4"),
    "xs": ("sbuf", [128, NC * N], "uint8"),
    "wq": ("sbuf", [128, NC * N], "float8_e4m3fn_x4"),
    "ws": ("sbuf", [128, NC * N], "uint8"),
    "acc": ("psum", [128, 512], "float32"),
    "yb": ("sbuf", [128, NC], "float32"),
}
SEMAPHORES = (["xl", "wl", "qx", "qw", "sent", "mm", "cp", "st"]
              + ["c%d" % j for j in range(N)]
              + ["p%d" % j for j in range(N)])


def _count(mask):
    return bin(mask).count("1")


def _roles(core, cores, topo):
    def near(c):
        return topo.host(c) == topo.host(core) and topo.chip(c) == topo.chip(core)
    peer = [c for c in cores if c != core and near(c)][0]
    far = [c for c in cores if not near(c)]
    twin = [c for c in far if topo.die(c) == topo.die(core)][0]
    cross = [c for c in far if c != twin][0]
    leave = topo.mask(core, twin) & topo.mask(core, cross)
    stay = topo.mask(core, peer) & ~leave
    return peer, twin, cross, leave, stay


def rank_program(g, core, T, topo):
    rank = T.rank_of(core)
    if rank is None:
        return
    sem = T.sem
    peer, twin, cross, leave, stay = _roles(core, T.cores, topo)
    left = [0]

    def tile(j):
        return slice(NC * j, NC * (j + 1))

    def codes(j):
        return T.xq[:, tile(j)].bitcast(dt.uint8), sem["c%d" % j]

    def plane(j):
        return T.xs[:, tile(j)], sem["p%d" % j]

    def send(piece, where):
        view, arrived = piece
        transfers = []
        for dst, mask in where:
            rid, pid = topo.addr(dst, core)
            transfers.append(RemoteDMATransfer(dst_ids=[DstId(rid=rid, pnc=pid)], dma_engine_mask=mask,
                                               remote_sem=arrived, src=view, dst=view))
            left[0] += _count(mask)
        g.remote_dma_fused(transfers, local_sem=sem.sent)

    g.sync.dma_start(T.xb[:], T.x[:]).then_inc(sem.xl, 16)
    g.sync.dma_start(T.wb[:], T.w[:]).then_inc(sem.wl, 16)

    g.vector.wait_ge(sem.xl, 16)
    g.vector.quantize_mx(T.xq[:, tile(rank)], T.xs[:, tile(rank)], T.xb[:]).then_inc(sem.qx, 1)
    g.vector.wait_ge(sem.wl, 16)
    g.vector.quantize_mx(T.wq[:], T.ws[:], T.wb[:]).then_inc(sem.qw, 1)

    jt = T.rank_of(twin)
    g.wait_ge(sem.qx, 1)
    send(plane(rank), [(twin, leave)])
    send(codes(rank), [(twin, leave)])
    send(codes(rank), [(cross, leave), (peer, stay)])
    send(plane(rank), [(peer, stay)])
    g.wait_ge(sem["p%d" % jt], _count(_roles(twin, T.cores, topo)[3]))
    send(plane(jt), [(peer, stay)])

    _, _, _, p_leave, p_stay = _roles(peer, T.cores, topo)
    _, _, _, t_leave, _ = _roles(twin, T.cores, topo)
    _, _, _, c_leave, _ = _roles(cross, T.cores, topo)
    order = [(core, None),
             (peer, (_count(p_stay), _count(p_stay))),
             (twin, (_count(t_leave), _count(t_leave))),
             (cross, (_count(c_leave), _count(p_stay)))]
    g.tensor.wait_ge(sem.qx, 1)
    g.tensor.wait_ge(sem.qw, 1)
    for i, (c, need) in enumerate(order):
        j = T.rank_of(c)
        if need is not None:
            g.tensor.wait_ge(sem["c%d" % j], need[0])
            g.tensor.wait_ge(sem["p%d" % j], need[1])
        mm = g.tensor.matmul_mx(T.acc[:, 0:NC], T.wq[:, tile(j)], T.ws[:, tile(j)], T.xq[:, tile(j)], T.xs[:, tile(j)],
                                i == 0, i == N - 1)
    mm.then_inc(sem.mm, 1)

    g.vector.wait_ge(sem.mm, 1)
    g.vector.tensor_copy(T.yb[:], T.acc[:, 0:NC]).then_inc(sem.cp, 1)
    g.sync.wait_ge(sem.cp, 1)
    g.sync.dma_start(T.y[:], T.yb[:]).then_inc(sem.st, 16)
    g.sync.wait_ge(sem.st, 16)

    g.wait_ge(sem.sent, left[0])
